import numpy as np
import ml_dtypes


def mxq(x, axis, fmt="e4m3"):
    dtype, down = {"e4m3": (ml_dtypes.float8_e4m3fn, 7), "e5m2": (ml_dtypes.float8_e5m2, 14)}[fmt]
    v = np.moveaxis(np.asarray(x, np.float32).astype(ml_dtypes.bfloat16).astype(np.float64), axis, -1)
    blocks = v.reshape(v.shape[:-1] + (-1, 32))
    amax = np.abs(blocks).max(-1, keepdims=True)
    byte = np.maximum(np.where(amax > 0, np.frexp(amax)[1] - 1 + 127, 0) - down, 1)
    scale = np.exp2(byte - 127.0)
    codes = (blocks / scale).astype(np.float32).astype(dtype).astype(np.float64)
    return np.moveaxis((codes * scale).reshape(v.shape), -1, axis)


WIDE = False


def mx_kscale(k):
    if not WIDE:
        return np.ones(k)
    levels = np.array([30, -30])
    if k % 512:
        return np.exp2(np.random.permutation(np.resize(levels, k // 32))).repeat(32)
    a = np.empty((k // 512, 16))
    for p in range(k // 512):
        a[p, :8] = np.random.permutation(np.resize(levels, 8))
        for g in range(8):
            far = levels[np.abs(levels - a[p, g]) >= 10]
            a[p, g + 8] = far[np.random.randint(len(far))]
    return np.exp2(a.ravel()).repeat(32)


BF16 = ml_dtypes.bfloat16


def bf(x):
    return np.asarray(x, np.float32).astype(BF16)


def f64(x):
    return np.asarray(x).astype(np.float64)


E2M1 = np.array([0.0, 0.5, 1.0, 1.5, 2.0, 3.0, 4.0, 6.0, -0.0, -0.5, -1.0, -1.5, -2.0, -3.0, -4.0, -6.0])


def pack_weight(w, fmt):
    k, n = w.shape
    w = f64(bf(w)).reshape(k // 32, 32, n)
    amax = np.abs(w).max(1)
    if fmt in ("e4m3", "e5m2"):
        byte = np.frexp(amax)[1] - 1 + 127 - (7 if fmt == "e4m3" else 14)
    else:
        mant, ex = np.frexp(amax / 6.0)
        byte = np.where(mant > 0.5, ex, ex - 1) + 127
    byte = np.clip(np.where(amax > 0, byte, 1), 1, 254)
    scaled = (w * np.exp2(127.0 - byte)[:, None, :]).reshape(k, n).astype(np.float32)
    by_word = np.ascontiguousarray(scaled.reshape(k // 512, 128, 4, n).transpose(0, 1, 3, 2))
    if fmt in ("e4m3", "e5m2"):
        words = by_word.astype(ml_dtypes.float8_e4m3fn if fmt == "e4m3" else ml_dtypes.float8_e5m2).view(np.uint8)
    else:
        c = by_word.astype(ml_dtypes.float4_e2m1fn).view(np.uint8) & 0xF
        words = c[..., 0::2] | (c[..., 1::2] << 4)
    return np.ascontiguousarray(words), np.ascontiguousarray(byte.astype(np.uint8).reshape(k // 512, 16, n))


def unpack_weight(words, scales, fmt):
    g, p, n, _ = words.shape
    if fmt in ("e4m3", "e5m2"):
        vals = np.ascontiguousarray(words).view(ml_dtypes.float8_e4m3fn if fmt == "e4m3" else ml_dtypes.float8_e5m2).astype(np.float64)
    else:
        nib = np.empty((g, p, n, 4), np.uint8)
        nib[..., 0::2] = words & 0xF
        nib[..., 1::2] = words >> 4
        vals = E2M1[nib]
    vals = vals * np.repeat(np.exp2(scales.astype(np.float64) - 127.0), 8, axis=1)[..., None]
    return vals.transpose(0, 1, 3, 2).reshape(g * 512, n)


M, K, R = 1024, 2048, 512


def setup_inputs():
    s, t = mx_kscale(K), mx_kscale(M)
    tail = np.exp(0.5 * np.random.standard_normal((K, M)) - 0.25)
    e = f64(bf(2.4 / np.sqrt(K) * np.random.standard_normal((K, M)) * tail))
    g_words, g_scales = pack_weight(e * s[:, None], "e5m2")
    pair = np.exp(0.3 * np.random.standard_normal((M, M)))
    coef = 5.0 / np.sqrt(M) * np.random.standard_normal((M, R))
    return {"g_words": g_words,
            "g_scales": g_scales,
            "errs": bf((e / s[:, None]).T),
            "pair": bf(pair * t),
            "coef": bf(coef / t[:, None]),
            "lam": bf(0.3 * np.random.standard_normal(R))}


def reference(g_words, g_scales, errs, pair, coef, lam):
    g = unpack_weight(g_words, g_scales, "e5m2")
    f = mxq(f64(errs), 1, "e4m3")
    b = g.T @ f.T
    h = b * f64(pair)
    z = mxq(h, 1, "e5m2") @ mxq(f64(coef), 0, "e4m3")
    return z - f64(lam)

@@ -1,0 +1,347 @@
+from contextlib import ExitStack
+
+import concourse.mybir as mybir
+from concourse.masks import make_identity
+
+M, K, R = 1024, 2048, 512
+FLOPS = 2 * M * M * K + 2 * M * M * R
+BYTES = K * M + K * M // 32 + 2 * M * K + 2 * M * M + 2 * M * R + 2 * R + 4 * M * R
+
+F32 = mybir.dt.float32
+BF16 = mybir.dt.bfloat16
+U32 = mybir.dt.uint32
+I32 = mybir.dt.int32
+U8 = mybir.dt.uint8
+E4M3X4 = mybir.dt.float8_e4m3fn_x4
+E5M2X4 = mybir.dt.float8_e5m2_x4
+ALU = mybir.AluOpType
+
+P = 128
+PASS = 512
+GROUPS = K // PASS
+HALVES = M // PASS
+TILES = M // P
+BLOCKS = PASS // P
+
+
+def tile_weighted_diis_residuals_e3_kernel(tc, g_words, g_scales, errs, pair, coef, lam, out):
+    nc = tc.nc
+    with ExitStack() as ctx:
+        keep = ctx.enter_context(tc.tile_pool(name="keep", bufs=1))
+        stage = ctx.enter_context(tc.tile_pool(name="stage", bufs=4))
+        turn_psum = ctx.enter_context(tc.psum_pool(name="turn_psum", bufs=4))
+        acc_psum = ctx.enter_context(tc.psum_pool(name="acc_psum", bufs=4))
+        ctx.enter_context(tc.manual_schedule())
+
+        g_code = [keep.tile([P, GROUPS, PASS], U32, align_bytes=64, name=f"g_code{h}") for h in range(2)]
+        g_plane = keep.tile([P, GROUPS, M], U8, align_bytes=64, name="g_plane")
+        pair_sb = [keep.tile([P, BLOCKS, M], BF16, align_bytes=64, name=f"pair{h}") for h in range(2)]
+        coef_raw = keep.tile([P, HALVES, 4, R], BF16, align_bytes=64, name="coef_raw")
+        coef_quads = [keep.tile([P, R, 4], BF16, align_bytes=64, name=f"coef_quads{j}") for j in range(HALVES)]
+        coef_code = [keep.tile([P, R], U32, align_bytes=64, name=f"coef_code{j}") for j in range(HALVES)]
+        coef_plane = [keep.tile([P, R], U8, align_bytes=64, name=f"coef_plane{j}") for j in range(HALVES)]
+        lam_sb = keep.tile([P, R], BF16, align_bytes=64, name="lam_sb")
+        ident = keep.tile([P, P], F32, align_bytes=64, name="ident")
+        e_code = [[keep.tile([P, PASS], U32, align_bytes=64, name=f"e_code{j}{g}") for g in range(GROUPS)] for j in range(HALVES)]
+        e_plane = [[keep.tile([P, PASS], U8, align_bytes=64, name=f"e_plane{j}{g}") for g in range(GROUPS)] for j in range(HALVES)]
+        h_code = [[keep.tile([P, 2 * P], U32, align_bytes=64, name=f"h_code{j}{q}") for q in range(4)] for j in range(HALVES)]
+        h_plane = [[keep.tile([P, 2 * P], U8, align_bytes=64, name=f"h_plane{j}{q}") for q in range(4)] for j in range(HALVES)]
+        h_sb = [[keep.tile([P, PASS], BF16, align_bytes=64, name=f"h{j}{i}") for i in range(TILES)] for j in range(HALVES)]
+
+        nc.vector.memset(g_plane[:].bitcast(I32), 0)
+        make_identity(nc, ident[:])
+
+        e_raw = {}
+
+        def load_errs(j, rt):
+            t = keep.tile([P, K], BF16, align_bytes=64, name=f"e_raw{j}{rt}")
+            nc.sync.dma_start(out=t[:], in_=errs[j * PASS + rt * P : j * PASS + (rt + 1) * P, :])
+            e_raw[j, rt] = t
+
+        def load_g(h, g0, n):
+            nc.sync.dma_start(
+                out=g_code[h][:, g0 : g0 + n, :].bitcast(I32),
+                in_=g_words[g0 : g0 + n].rearrange("g p n t -> p g (n t)")[:, :, h * 4 * PASS : (h + 1) * 4 * PASS].bitcast(I32),
+            )
+        def load_scales():
+            for quad in range(4):
+                nc.sync.dma_start(
+                    out=g_plane[32 * quad : 32 * quad + 4, :, :].bitcast(I32),
+                    in_=g_scales[:, 4 * quad : 4 * quad + 4, :].rearrange("g r n -> r g n").bitcast(I32),
+                )
+
+        def load_pair(h, j0, n):
+            nc.sync.dma_start(
+                out=pair_sb[h][:, :, j0 * PASS : (j0 + n) * PASS],
+                in_=pair[h * PASS : (h + 1) * PASS, j0 * PASS : (j0 + n) * PASS].rearrange("(i p) j -> p i j", p=P),
+            )
+
+        def load_coef():
+            nc.sync.dma_start(out=coef_raw[:], in_=coef.rearrange("(j p t) r -> p j t r", p=P, t=4))
+
+        def load_lam():
+            nc.sync.dma_start(out=lam_sb[:], in_=lam.partition_broadcast(P))
+
+        load_errs(0, 0)
+        load_errs(0, 1)
+        load_errs(0, 2)
+        load_scales()
+        load_errs(0, 3)
+        load_g(0, 0, 2)
+        load_g(0, 2, 2)
+        load_pair(0, 0, 1)
+        load_g(1, 0, 2)
+        load_g(1, 2, 2)
+        load_errs(1, 0)
+        load_errs(1, 1)
+        load_pair(1, 0, 1)
+        load_errs(1, 2)
+        load_errs(1, 3)
+        load_pair(0, 1, 1)
+        load_pair(1, 1, 1)
+        load_coef()
+        load_lam()
+
+        split = {}
+        e_quads = {}
+
+        def move(engine, dst, src):
+            if engine == "V":
+                nc.vector.tensor_copy(out=dst, in_=src)
+            else:
+                nc.scalar.copy(out=dst, in_=src)
+
+        def quad_words(quads, col):
+            words = quads.rearrange("p b n t -> p b (n t)").bitcast(F32)
+            return words[:, :, 2 * col : 2 * (col + P)].rearrange("p b (r u) -> p b r u", u=2)
+
+        def shuf(j, rt, kh, engine):
+            t = stage.tile([P, 2, 2, P], F32, align_bytes=64, name="split", bufs=8)
+            src = e_raw[j, rt][:].bitcast(F32)[:, kh * PASS : (kh + 1) * PASS].rearrange("p (g w u) -> p g u w", g=2, u=2)
+            move(engine, t[:], src)
+            split[j, rt, kh] = t
+
+        def turn(j, rt, kh, engine):
+            if (j, kh) not in e_quads:
+                e_quads[j, kh] = keep.tile([P, 2, PASS, 4], BF16, align_bytes=64, name=f"e_quads{j}{kh}")
+            bank = turn_psum.tile([P, 4, P], F32, name="turn")
+            for g in range(2):
+                for u in range(2):
+                    if (j, rt, kh) in split:
+                        word = split[j, rt, kh][:, g, u, :]
+                    else:
+                        w0 = kh * PASS + g * 2 * P
+                        word = e_raw[j, rt][:].bitcast(F32)[:, w0 + u : w0 + 2 * P : 2]
+                    nc.tensor.transpose(bank[:, 2 * g + u, :], word, ident[:])
+            move(engine, quad_words(e_quads[j, kh][:], rt * P), bank[:].rearrange("p (b u) r -> p b r u", u=2))
+
+        def quant(j, g, c):
+            cols = slice(2 * c * P, 2 * (c + 1) * P)
+            nc.vector.quantize_mx(
+                out=e_code[j][g][:, cols].bitcast(E4M3X4),
+                scales=e_plane[j][g][:, cols],
+                in_=e_quads[j, g // 2][:, g % 2, cols, :].rearrange("p n t -> p (n t)"),
+            )
+
+        accs = {}
+
+        def overlap(j, i, g):
+            if g == 0:
+                accs[j, i] = acc_psum.tile([P, PASS], F32, name="acc")
+            cols = slice((i % BLOCKS) * P, (i % BLOCKS + 1) * P)
+            nc.tensor.matmul_mx(
+                out=accs[j, i][:],
+                lhsT=g_code[i // BLOCKS][:, g, cols].bitcast(E5M2X4),
+                lhsT_scale=g_plane[:, g, i * P : (i + 1) * P],
+                rhs=e_code[j][g][:].bitcast(E4M3X4),
+                rhs_scale=e_plane[j][g][:],
+                start=(g == 0),
+                stop=(g == GROUPS - 1),
+            )
+
+        def units(j, i, part):
+            for g in {"A": (0, 1), "B": (2, 3), "F": (0, 1, 2, 3)}[part]:
+                overlap(j, i, g)
+
+        def weight(j, i):
+            nc.vector.tensor_tensor(
+                out=h_sb[j][i][:].rearrange("p (u w e) -> p u w e", u=2, e=2),
+                in0=accs[j, i][:].rearrange("p (w u e) -> p u w e", u=2, e=2),
+                in1=pair_sb[i // BLOCKS][:, i % BLOCKS, j * PASS : (j + 1) * PASS].rearrange("p (w u e) -> p u w e", u=2, e=2),
+                op=ALU.mult,
+            )
+
+        h_bank = {}
+        h_quads = {}
+
+        def turn_h(j, i):
+            q, a = divmod(i, 2)
+            if (j, q) not in h_bank:
+                h_bank[j, q] = turn_psum.tile([P, 4, P], F32, name="turn")
+            words = h_sb[j][i][:].bitcast(F32)
+            for u in range(2):
+                nc.tensor.transpose(h_bank[j, q][:, 2 * a + u, :], words[:, u * P : (u + 1) * P], ident[:])
+
+        def out_h(j, q, engine="A"):
+            h_quads[j, q] = stage.tile([P, 2, P, 4], BF16, align_bytes=64, name="h_quads", bufs=8)
+            move(engine, quad_words(h_quads[j, q][:], 0), h_bank[j, q][:].rearrange("p (b u) r -> p b r u", u=2))
+
+        def quant_h(j, q):
+            nc.vector.quantize_mx(
+                out=h_code[j][q][:].bitcast(E5M2X4), scales=h_plane[j][q][:], in_=h_quads[j, q][:].rearrange("p b n t -> p (b n t)")
+            )
+
+        def coef_copy(j, c, engine="A"):
+            cols = slice(c * R // 2, (c + 1) * R // 2)
+            move(engine, coef_quads[j][:, cols, :], coef_raw[:, j, :, cols].rearrange("p t n -> p n t"))
+
+        def coef_quantize(j):
+            nc.vector.quantize_mx(
+                out=coef_code[j][:].bitcast(E4M3X4), scales=coef_plane[j][:], in_=coef_quads[j][:].rearrange("p n t -> p (n t)")
+            )
+
+        def zmm(i):
+            accs[2, i] = acc_psum.tile([P, PASS], F32, name="acc")
+            cols = slice((i % 2) * P, (i % 2 + 1) * P)
+            for j in range(HALVES):
+                nc.tensor.matmul_mx(
+                    out=accs[2, i][:],
+                    lhsT=h_code[j][i // 2][:, cols].bitcast(E5M2X4),
+                    lhsT_scale=h_plane[j][i // 2][:, cols],
+                    rhs=coef_code[j][:].bitcast(E4M3X4),
+                    rhs_scale=coef_plane[j][:],
+                    start=(j == 0),
+                    stop=(j == HALVES - 1),
+                )
+
+        def store(i):
+            res = keep.tile([P, R], F32, align_bytes=64, name=f"res{i}")
+            nc.vector.tensor_tensor(out=res[:], in0=accs[2, i][:], in1=lam_sb[:], op=ALU.subtract)
+            nc.sync.dma_start(out=out[i * P : (i + 1) * P, :], in_=res[:])
+
+        turn(0, 1, 0, "V")
+        turn(0, 0, 0, "A")
+        turn(0, 1, 1, "A")
+        turn(0, 0, 1, "V")
+        turn(0, 2, 1, "A")
+        turn(0, 2, 0, "V")
+        turn(0, 3, 0, "A")
+        turn(0, 3, 1, "A")
+        shuf(1, 0, 1, "A")
+        quant(0, 1, 0)
+        shuf(1, 0, 0, "A")
+        quant(0, 2, 0)
+        shuf(1, 1, 0, "A")
+        quant(0, 0, 0)
+        quant(0, 3, 0)
+        quant(0, 0, 1)
+        quant(0, 1, 1)
+        quant(0, 2, 1)
+        quant(0, 3, 1)
+        units(0, 2, "F")
+        units(0, 0, "F")
+        units(0, 1, "F")
+        weight(0, 2)
+        units(0, 6, "F")
+        weight(0, 1)
+        units(0, 5, "F")
+        weight(0, 0)
+        turn(1, 0, 1, "A")
+        shuf(1, 1, 1, "V")
+        turn(1, 0, 0, "V")
+        weight(0, 5)
+        turn(1, 1, 1, "A")
+        shuf(1, 2, 1, "V")
+        turn(1, 1, 0, "A")
+        shuf(1, 2, 0, "A")
+        shuf(1, 3, 0, "A")
+        units(0, 7, "F")
+        units(0, 4, "F")
+        quant(1, 3, 0)
+        shuf(1, 3, 1, "V")
+        turn(1, 2, 1, "A")
+        quant(1, 2, 0)
+        turn(1, 2, 0, "A")
+        weight(0, 6)
+        turn(1, 3, 1, "A")
+        weight(0, 4)
+        quant(1, 1, 0)
+        quant(1, 0, 0)
+        turn(1, 3, 0, "A")
+        weight(0, 7)
+        units(0, 3, "F")
+        quant(1, 0, 1)
+        turn_h(0, 0)
+        turn_h(0, 4)
+        turn_h(0, 5)
+        quant(1, 1, 1)
+        quant(1, 2, 1)
+        turn_h(0, 6)
+        quant(1, 3, 1)
+        turn_h(0, 1)
+        turn_h(0, 7)
+        out_h(0, 2, "A")
+        weight(0, 3)
+        units(1, 3, "F")
+        units(1, 2, "F")
+        coef_copy(0, 1, "V")
+        units(1, 4, "F")
+        out_h(0, 0, "V")
+        coef_copy(0, 0, "V")
+        weight(1, 3)
+        weight(1, 2)
+        units(1, 0, "F")
+        weight(1, 0)
+        units(1, 1, "F")
+        weight(1, 4)
+        coef_copy(1, 0, "A")
+        out_h(0, 3, "A")
+        quant_h(0, 3)
+        units(1, 5, "F")
+        units(1, 6, "F")
+        weight(1, 1)
+        turn_h(0, 2)
+        coef_copy(1, 1, "A")
+        turn_h(1, 0)
+        coef_quantize(0)
+        turn_h(0, 3)
+        weight(1, 5)
+        turn_h(1, 2)
+        quant_h(0, 0)
+        turn_h(1, 1)
+        out_h(0, 1, "A")
+        quant_h(0, 2)
+        turn_h(1, 3)
+        coef_quantize(1)
+        turn_h(1, 4)
+        weight(1, 6)
+        turn_h(1, 5)
+        out_h(1, 1, "A")
+        out_h(1, 2, "A")
+        units(1, 7, "F")
+        quant_h(0, 1)
+        quant_h(1, 1)
+        zmm(2)
+        quant_h(1, 2)
+        zmm(4)
+        out_h(1, 0, "A")
+        weight(1, 7)
+        turn_h(1, 6)
+        store(2)
+        turn_h(1, 7)
+        zmm(5)
+        quant_h(1, 0)
+        zmm(0)
+        out_h(1, 3, "A")
+        store(4)
+        store(5)
+        quant_h(1, 3)
+        zmm(1)
+        store(0)
+        store(1)
+        zmm(6)
+        zmm(3)
+        store(6)
+        store(3)
+        zmm(7)
+        store(7)

@@ -33,9 +33,9 @@ def tile_weighted_diis_residuals_e3_kernel(tc, g_words, g_scales, errs, pair, co
         acc_psum = ctx.enter_context(tc.psum_pool(name="acc_psum", bufs=4))
         ctx.enter_context(tc.manual_schedule())
 
-        g_code = [keep.tile([P, GROUPS, PASS], U32, align_bytes=64, name=f"g_code{h}") for h in range(2)]
+        g_code = {}
         g_plane = keep.tile([P, GROUPS, M], U8, align_bytes=64, name="g_plane")
-        pair_sb = [keep.tile([P, BLOCKS, M], BF16, align_bytes=64, name=f"pair{h}") for h in range(2)]
+        pair_sb = {}
         coef_raw = keep.tile([P, HALVES, 4, R], BF16, align_bytes=64, name="coef_raw")
         coef_quads = [keep.tile([P, R, 4], BF16, align_bytes=64, name=f"coef_quads{j}") for j in range(HALVES)]
         coef_code = [keep.tile([P, R], U32, align_bytes=64, name=f"coef_code{j}") for j in range(HALVES)]
@@ -48,8 +48,27 @@ def tile_weighted_diis_residuals_e3_kernel(tc, g_words, g_scales, errs, pair, co
         h_plane = [[keep.tile([P, 2 * P], U8, align_bytes=64, name=f"h_plane{j}{q}") for q in range(4)] for j in range(HALVES)]
         h_sb = [[keep.tile([P, PASS], BF16, align_bytes=64, name=f"h{j}{i}") for i in range(TILES)] for j in range(HALVES)]
 
-        nc.vector.memset(g_plane[:].bitcast(I32), 0)
         make_identity(nc, ident[:])
+
+        def warm_setup():
+            zero = keep.tile([P, 4 * PASS], BF16, align_bytes=64, name="zero")
+            wm = keep.tile([P, PASS], U32, align_bytes=64, name="warm_moving")
+            wmp = keep.tile([P, PASS], U8, align_bytes=64, name="warm_moving_plane")
+            ws = keep.tile([P, P], U32, align_bytes=64, name="warm_stationary")
+            wsp = keep.tile([P, P], U8, align_bytes=64, name="warm_stationary_plane")
+            nc.vector.memset(zero[:], 0.0)
+            nc.vector.memset(g_plane[:].bitcast(I32), 0)
+            nc.vector.quantize_mx(out=wm[:].bitcast(E4M3X4), scales=wmp[:], in_=zero[:])
+            nc.vector.quantize_mx(out=ws[:].bitcast(E5M2X4), scales=wsp[:], in_=zero[:, : 4 * P])
+            return wm, wmp, ws, wsp
+
+        def warm(n):
+            wm, wmp, ws, wsp = warm_tiles
+            bank = acc_psum.tile([P, PASS], F32, name="acc")
+            for w in range(n):
+                nc.tensor.matmul_mx(out=bank[:], lhsT=ws[:].bitcast(E5M2X4), lhsT_scale=wsp[:], rhs=wm[:].bitcast(E4M3X4), rhs_scale=wmp[:], start=True, stop=True)
+
+        warm_tiles = warm_setup()
 
         e_raw = {}
 
@@ -58,11 +77,15 @@ def tile_weighted_diis_residuals_e3_kernel(tc, g_words, g_scales, errs, pair, co
             nc.sync.dma_start(out=t[:], in_=errs[j * PASS + rt * P : j * PASS + (rt + 1) * P, :])
             e_raw[j, rt] = t
 
-        def load_g(h, g0, n):
+        def load_g(i0, ni, g0, ng):
+            t = keep.tile([P, ng, ni * P], U32, align_bytes=64, name=f"g_code{i0}{g0}")
             nc.sync.dma_start(
-                out=g_code[h][:, g0 : g0 + n, :].bitcast(I32),
-                in_=g_words[g0 : g0 + n].rearrange("g p n t -> p g (n t)")[:, :, h * 4 * PASS : (h + 1) * 4 * PASS].bitcast(I32),
+                out=t[:].bitcast(I32),
+                in_=g_words[g0 : g0 + ng].rearrange("g p n t -> p g (n t)")[:, :, i0 * 4 * P : (i0 + ni) * 4 * P].bitcast(I32),
             )
+            for i in range(i0, i0 + ni):
+                for g in range(g0, g0 + ng):
+                    g_code[i, g] = (t, g0, i0)
         def load_scales():
             for quad in range(4):
                 nc.sync.dma_start(
@@ -70,10 +93,11 @@ def tile_weighted_diis_residuals_e3_kernel(tc, g_words, g_scales, errs, pair, co
                     in_=g_scales[:, 4 * quad : 4 * quad + 4, :].rearrange("g r n -> r g n").bitcast(I32),
                 )
 
-        def load_pair(h, j0, n):
+        def load_pair(h, j):
+            pair_sb[h, j] = keep.tile([P, BLOCKS, PASS], BF16, align_bytes=64, name=f"pair{h}{j}")
             nc.sync.dma_start(
-                out=pair_sb[h][:, :, j0 * PASS : (j0 + n) * PASS],
-                in_=pair[h * PASS : (h + 1) * PASS, j0 * PASS : (j0 + n) * PASS].rearrange("(i p) j -> p i j", p=P),
+                out=pair_sb[h, j][:],
+                in_=pair[h * PASS : (h + 1) * PASS, j * PASS : (j + 1) * PASS].rearrange("(i p) j -> p i j", p=P),
             )
 
         def load_coef():
@@ -83,22 +107,22 @@ def tile_weighted_diis_residuals_e3_kernel(tc, g_words, g_scales, errs, pair, co
             nc.sync.dma_start(out=lam_sb[:], in_=lam.partition_broadcast(P))
 
         load_errs(0, 0)
+        load_scales()
         load_errs(0, 1)
         load_errs(0, 2)
-        load_scales()
         load_errs(0, 3)
-        load_g(0, 0, 2)
-        load_g(0, 2, 2)
-        load_pair(0, 0, 1)
-        load_g(1, 0, 2)
-        load_g(1, 2, 2)
+        load_g(0, 8, 0, 1)
+        load_g(0, 8, 1, 1)
+        load_g(0, 8, 2, 1)
+        load_g(0, 8, 3, 1)
+        load_pair(0, 0)
         load_errs(1, 0)
         load_errs(1, 1)
-        load_pair(1, 0, 1)
+        load_pair(1, 0)
         load_errs(1, 2)
         load_errs(1, 3)
-        load_pair(0, 1, 1)
-        load_pair(1, 1, 1)
+        load_pair(0, 1)
+        load_pair(1, 1)
         load_coef()
         load_lam()
 
@@ -112,8 +136,10 @@ def tile_weighted_diis_residuals_e3_kernel(tc, g_words, g_scales, errs, pair, co
                 nc.scalar.copy(out=dst, in_=src)
 
         def quad_words(quads, col):
-            words = quads.rearrange("p b n t -> p b (n t)").bitcast(F32)
-            return words[:, :, 2 * col : 2 * (col + P)].rearrange("p b (r u) -> p b r u", u=2)
+            words = quads.rearrange("p n t -> p (n t)").bitcast(F32)
+            return words[:, 2 * col : 2 * (col + 2 * P)].rearrange("p (b r u) -> p b r u", b=2, u=2)
+
+        e_bank = {}
 
         def shuf(j, rt, kh, engine):
             t = stage.tile([P, 2, 2, P], F32, align_bytes=64, name="split", bufs=8)
@@ -121,26 +147,28 @@ def tile_weighted_diis_residuals_e3_kernel(tc, g_words, g_scales, errs, pair, co
             move(engine, t[:], src)
             split[j, rt, kh] = t
 
-        def turn(j, rt, kh, engine):
-            if (j, kh) not in e_quads:
-                e_quads[j, kh] = keep.tile([P, 2, PASS, 4], BF16, align_bytes=64, name=f"e_quads{j}{kh}")
-            bank = turn_psum.tile([P, 4, P], F32, name="turn")
-            for g in range(2):
-                for u in range(2):
-                    if (j, rt, kh) in split:
-                        word = split[j, rt, kh][:, g, u, :]
-                    else:
-                        w0 = kh * PASS + g * 2 * P
-                        word = e_raw[j, rt][:].bitcast(F32)[:, w0 + u : w0 + 2 * P : 2]
-                    nc.tensor.transpose(bank[:, 2 * g + u, :], word, ident[:])
-            move(engine, quad_words(e_quads[j, kh][:], rt * P), bank[:].rearrange("p (b u) r -> p b r u", u=2))
+        def turn(j, g, rt):
+            if (j, g, rt // 2) not in e_bank:
+                bank = turn_psum.tile([P, 4, P], F32, name="turn")
+                e_bank[j, g, rt // 2] = bank
+            for u in range(2):
+                if (j, rt, g // 2) in split:
+                    word = split[j, rt, g // 2][:, g % 2, u, :]
+                else:
+                    word = e_raw[j, rt][:].bitcast(F32)[:, 2 * P * g + u : 2 * P * (g + 1) : 2]
+                nc.tensor.transpose(e_bank[j, g, rt // 2][:, 2 * (rt % 2) + u, :], word, ident[:])
+
+        def gather(j, g, c, engine):
+            if (j, g) not in e_quads:
+                e_quads[j, g] = keep.tile([P, PASS, 4], BF16, align_bytes=64, name=f"e_quads{j}{g}")
+            move(engine, quad_words(e_quads[j, g][:], 2 * c * P), e_bank[j, g, c][:].rearrange("p (b u) r -> p b r u", u=2))
 
         def quant(j, g, c):
             cols = slice(2 * c * P, 2 * (c + 1) * P)
             nc.vector.quantize_mx(
                 out=e_code[j][g][:, cols].bitcast(E4M3X4),
                 scales=e_plane[j][g][:, cols],
-                in_=e_quads[j, g // 2][:, g % 2, cols, :].rearrange("p n t -> p (n t)"),
+                in_=e_quads[j, g][:, cols, :].rearrange("p n t -> p (n t)"),
             )
 
         accs = {}
@@ -148,10 +176,10 @@ def tile_weighted_diis_residuals_e3_kernel(tc, g_words, g_scales, errs, pair, co
         def overlap(j, i, g):
             if g == 0:
                 accs[j, i] = acc_psum.tile([P, PASS], F32, name="acc")
-            cols = slice((i % BLOCKS) * P, (i % BLOCKS + 1) * P)
+            t, g0, i0 = g_code[i, g]
             nc.tensor.matmul_mx(
                 out=accs[j, i][:],
-                lhsT=g_code[i // BLOCKS][:, g, cols].bitcast(E5M2X4),
+                lhsT=t[:, g - g0, (i - i0) * P : (i - i0 + 1) * P].bitcast(E5M2X4),
                 lhsT_scale=g_plane[:, g, i * P : (i + 1) * P],
                 rhs=e_code[j][g][:].bitcast(E4M3X4),
                 rhs_scale=e_plane[j][g][:],
@@ -160,14 +188,14 @@ def tile_weighted_diis_residuals_e3_kernel(tc, g_words, g_scales, errs, pair, co
             )
 
         def units(j, i, part):
-            for g in {"A": (0, 1), "B": (2, 3), "F": (0, 1, 2, 3)}[part]:
+            for g in {"F": (0, 1, 2, 3), "0": (0,), "1": (1,), "2": (2,), "3": (3,)}[part]:
                 overlap(j, i, g)
 
         def weight(j, i):
             nc.vector.tensor_tensor(
                 out=h_sb[j][i][:].rearrange("p (u w e) -> p u w e", u=2, e=2),
                 in0=accs[j, i][:].rearrange("p (w u e) -> p u w e", u=2, e=2),
-                in1=pair_sb[i // BLOCKS][:, i % BLOCKS, j * PASS : (j + 1) * PASS].rearrange("p (w u e) -> p u w e", u=2, e=2),
+                in1=pair_sb[i // BLOCKS, j][:, i % BLOCKS, :].rearrange("p (w u e) -> p u w e", u=2, e=2),
                 op=ALU.mult,
             )
 
@@ -183,12 +211,12 @@ def tile_weighted_diis_residuals_e3_kernel(tc, g_words, g_scales, errs, pair, co
                 nc.tensor.transpose(h_bank[j, q][:, 2 * a + u, :], words[:, u * P : (u + 1) * P], ident[:])
 
         def out_h(j, q, engine="A"):
-            h_quads[j, q] = stage.tile([P, 2, P, 4], BF16, align_bytes=64, name="h_quads", bufs=8)
+            h_quads[j, q] = stage.tile([P, 2 * P, 4], BF16, align_bytes=64, name="h_quads", bufs=8)
             move(engine, quad_words(h_quads[j, q][:], 0), h_bank[j, q][:].rearrange("p (b u) r -> p b r u", u=2))
 
         def quant_h(j, q):
             nc.vector.quantize_mx(
-                out=h_code[j][q][:].bitcast(E5M2X4), scales=h_plane[j][q][:], in_=h_quads[j, q][:].rearrange("p b n t -> p (b n t)")
+                out=h_code[j][q][:].bitcast(E5M2X4), scales=h_plane[j][q][:], in_=h_quads[j, q][:].rearrange("p n t -> p (n t)")
             )
 
         def coef_copy(j, c, engine="A"):
@@ -214,134 +242,188 @@ def tile_weighted_diis_residuals_e3_kernel(tc, g_words, g_scales, errs, pair, co
                     stop=(j == HALVES - 1),
                 )
 
+        def store_last(i):
+            for c in range(2):
+                cols = slice(c * R // 2, (c + 1) * R // 2)
+                res = keep.tile([P, R // 2], F32, align_bytes=64, name=f"res_last{c}")
+                nc.vector.tensor_tensor(out=res[:], in0=accs[2, i][:, cols], in1=lam_sb[:, cols], op=ALU.subtract)
+                nc.sync.dma_start(out=out[i * P : (i + 1) * P, cols], in_=res[:])
+
         def store(i):
             res = keep.tile([P, R], F32, align_bytes=64, name=f"res{i}")
             nc.vector.tensor_tensor(out=res[:], in0=accs[2, i][:], in1=lam_sb[:], op=ALU.subtract)
             nc.sync.dma_start(out=out[i * P : (i + 1) * P, :], in_=res[:])
 
-        turn(0, 1, 0, "V")
-        turn(0, 0, 0, "A")
-        turn(0, 1, 1, "A")
-        turn(0, 0, 1, "V")
-        turn(0, 2, 1, "A")
-        turn(0, 2, 0, "V")
-        turn(0, 3, 0, "A")
-        turn(0, 3, 1, "A")
-        shuf(1, 0, 1, "A")
-        quant(0, 1, 0)
-        shuf(1, 0, 0, "A")
-        quant(0, 2, 0)
-        shuf(1, 1, 0, "A")
+        warm(3)
+        turn(0, 1, 0)
+        turn(0, 0, 0)
+        turn(0, 2, 0)
+        turn(0, 3, 0)
+        warm(1)
+        turn(0, 0, 1)
+        turn(0, 1, 1)
+        turn(0, 3, 1)
+        turn(0, 2, 1)
+        gather(0, 1, 0, "V")
+        gather(0, 3, 0, "A")
+        gather(0, 0, 0, "V")
+        warm(1)
+        turn(0, 0, 2)
+        gather(0, 2, 0, "A")
         quant(0, 0, 0)
-        quant(0, 3, 0)
+        turn(0, 0, 3)
+        quant(0, 1, 0)
+        turn(0, 3, 2)
+        turn(0, 1, 2)
+        gather(0, 0, 1, "V")
+        turn(0, 2, 2)
+        turn(0, 2, 3)
+        turn(0, 1, 3)
         quant(0, 0, 1)
+        turn(0, 3, 3)
+        gather(0, 2, 1, "A")
+        gather(0, 1, 1, "V")
+        units(0, 0, "0")
+        gather(0, 3, 1, "A")
+        units(0, 3, "0")
+        quant(0, 2, 0)
+        units(0, 2, "0")
         quant(0, 1, 1)
+        units(0, 1, "0")
         quant(0, 2, 1)
+        units(0, 0, "1")
+        quant(0, 3, 0)
+        units(0, 3, "1")
         quant(0, 3, 1)
-        units(0, 2, "F")
-        units(0, 0, "F")
-        units(0, 1, "F")
-        weight(0, 2)
-        units(0, 6, "F")
-        weight(0, 1)
-        units(0, 5, "F")
+        units(0, 0, "2")
+        units(0, 2, "1")
+        units(0, 3, "2")
+        units(0, 0, "3")
+        units(0, 2, "2")
+        units(0, 2, "3")
+        units(0, 1, "1")
+        units(0, 3, "3")
         weight(0, 0)
-        turn(1, 0, 1, "A")
-        shuf(1, 1, 1, "V")
-        turn(1, 0, 0, "V")
-        weight(0, 5)
-        turn(1, 1, 1, "A")
-        shuf(1, 2, 1, "V")
-        turn(1, 1, 0, "A")
-        shuf(1, 2, 0, "A")
-        shuf(1, 3, 0, "A")
-        units(0, 7, "F")
-        units(0, 4, "F")
-        quant(1, 3, 0)
-        shuf(1, 3, 1, "V")
-        turn(1, 2, 1, "A")
-        quant(1, 2, 0)
-        turn(1, 2, 0, "A")
-        weight(0, 6)
-        turn(1, 3, 1, "A")
-        weight(0, 4)
-        quant(1, 1, 0)
-        quant(1, 0, 0)
-        turn(1, 3, 0, "A")
-        weight(0, 7)
-        units(0, 3, "F")
-        quant(1, 0, 1)
-        turn_h(0, 0)
-        turn_h(0, 4)
-        turn_h(0, 5)
-        quant(1, 1, 1)
-        quant(1, 2, 1)
-        turn_h(0, 6)
-        quant(1, 3, 1)
-        turn_h(0, 1)
-        turn_h(0, 7)
-        out_h(0, 2, "A")
+        units(0, 1, "2")
+        units(0, 1, "3")
         weight(0, 3)
-        units(1, 3, "F")
-        units(1, 2, "F")
-        coef_copy(0, 1, "V")
-        units(1, 4, "F")
-        out_h(0, 0, "V")
-        coef_copy(0, 0, "V")
-        weight(1, 3)
-        weight(1, 2)
-        units(1, 0, "F")
-        weight(1, 0)
-        units(1, 1, "F")
-        weight(1, 4)
-        coef_copy(1, 0, "A")
-        out_h(0, 3, "A")
-        quant_h(0, 3)
-        units(1, 5, "F")
-        units(1, 6, "F")
-        weight(1, 1)
+        weight(0, 1)
+        shuf(1, 0, 1, "A")
+        units(0, 4, "F")
+        weight(0, 2)
+        shuf(1, 0, 0, "V")
+        shuf(1, 1, 1, "A")
+        shuf(1, 1, 0, "V")
+        units(0, 5, "F")
+        turn(1, 1, 0)
+        turn(1, 2, 0)
+        turn(1, 2, 1)
+        turn(1, 1, 1)
+        weight(0, 5)
+        turn(1, 3, 0)
+        turn_h(0, 0)
+        turn(1, 3, 1)
+        gather(1, 1, 0, "V")
+        turn_h(0, 1)
+        gather(1, 3, 0, "A")
+        gather(1, 2, 0, "V")
+        out_h(0, 0, "A")
+        shuf(1, 2, 0, "V")
+        units(0, 6, "F")
+        shuf(1, 2, 1, "V")
+        turn(1, 0, 0)
+        shuf(1, 3, 0, "V")
+        turn(1, 0, 2)
+        turn(1, 0, 1)
+        shuf(1, 3, 1, "V")
+        turn(1, 1, 2)
+        turn(1, 2, 2)
+        quant(1, 3, 0)
+        gather(1, 0, 0, "A")
+        turn(1, 1, 3)
+        turn(1, 2, 3)
+        weight(0, 4)
+        turn(1, 0, 3)
+        gather(1, 0, 1, "A")
+        gather(1, 2, 1, "V")
+        gather(1, 1, 1, "A")
+        quant(1, 0, 0)
+        units(0, 7, "F")
+        quant(1, 0, 1)
+        turn(1, 3, 2)
+        quant(1, 1, 0)
+        turn(1, 3, 3)
         turn_h(0, 2)
-        coef_copy(1, 1, "A")
-        turn_h(1, 0)
-        coef_quantize(0)
+        quant(1, 1, 1)
+        turn_h(0, 4)
+        gather(1, 3, 1, "A")
+        turn_h(0, 5)
+        quant(1, 2, 0)
         turn_h(0, 3)
-        weight(1, 5)
-        turn_h(1, 2)
+        quant(1, 2, 1)
+        out_h(0, 2, "A")
+        quant(1, 3, 1)
+        weight(0, 6)
+        units(1, 1, "F")
+        coef_copy(1, 0, "A")
+        coef_copy(0, 0, "V")
+        units(1, 3, "F")
+        weight(0, 7)
         quant_h(0, 0)
-        turn_h(1, 1)
+        coef_copy(0, 1, "A")
+        weight(1, 3)
+        units(1, 2, "F")
+        weight(1, 1)
+        coef_copy(1, 1, "A")
+        coef_quantize(0)
+        units(1, 5, "F")
+        weight(1, 2)
         out_h(0, 1, "A")
-        quant_h(0, 2)
-        turn_h(1, 3)
+        units(1, 0, "F")
         coef_quantize(1)
-        turn_h(1, 4)
-        weight(1, 6)
-        turn_h(1, 5)
-        out_h(1, 1, "A")
-        out_h(1, 2, "A")
+        weight(1, 0)
         units(1, 7, "F")
         quant_h(0, 1)
-        quant_h(1, 1)
-        zmm(2)
-        quant_h(1, 2)
-        zmm(4)
-        out_h(1, 0, "A")
+        turn_h(1, 2)
+        weight(1, 5)
+        turn_h(0, 6)
+        turn_h(1, 3)
+        turn_h(0, 7)
+        turn_h(1, 0)
         weight(1, 7)
-        turn_h(1, 6)
-        store(2)
-        turn_h(1, 7)
-        zmm(5)
+        turn_h(1, 1)
+        quant_h(0, 2)
+        out_h(1, 0, "A")
+        out_h(1, 1, "A")
+        units(1, 6, "F")
         quant_h(1, 0)
+        out_h(0, 3, "A")
+        weight(1, 6)
+        units(1, 4, "F")
+        quant_h(0, 3)
         zmm(0)
-        out_h(1, 3, "A")
-        store(4)
-        store(5)
-        quant_h(1, 3)
-        zmm(1)
+        weight(1, 4)
+        turn_h(1, 6)
+        turn_h(1, 7)
         store(0)
-        store(1)
-        zmm(6)
+        turn_h(1, 4)
+        turn_h(1, 5)
+        out_h(1, 3, "A")
+        quant_h(1, 1)
+        zmm(1)
+        out_h(1, 2, "A")
+        quant_h(1, 3)
         zmm(3)
-        store(6)
-        store(3)
+        store(1)
         zmm(7)
+        quant_h(1, 2)
+        store(3)
+        zmm(4)
         store(7)
+        zmm(2)
+        store(4)
+        zmm(5)
+        store(2)
+        zmm(6)
+        store(5)
+        store_last(6)

@@ -29,8 +29,7 @@ def tile_weighted_diis_residuals_e3_kernel(tc, g_words, g_scales, errs, pair, co
     with ExitStack() as ctx:
         keep = ctx.enter_context(tc.tile_pool(name="keep", bufs=1))
         stage = ctx.enter_context(tc.tile_pool(name="stage", bufs=4))
-        turn_psum = ctx.enter_context(tc.psum_pool(name="turn_psum", bufs=4))
-        acc_psum = ctx.enter_context(tc.psum_pool(name="acc_psum", bufs=4))
+        psum = ctx.enter_context(tc.psum_pool(name="psum", bufs=8))
         ctx.enter_context(tc.manual_schedule())
 
         g_code = {}
@@ -51,20 +50,22 @@ def tile_weighted_diis_residuals_e3_kernel(tc, g_words, g_scales, errs, pair, co
         make_identity(nc, ident[:])
 
         def warm_setup():
-            zero = keep.tile([P, 4 * PASS], BF16, align_bytes=64, name="zero")
+            zero = keep.tile([P, PASS], BF16, align_bytes=64, name="zero")
             wm = keep.tile([P, PASS], U32, align_bytes=64, name="warm_moving")
             wmp = keep.tile([P, PASS], U8, align_bytes=64, name="warm_moving_plane")
             ws = keep.tile([P, P], U32, align_bytes=64, name="warm_stationary")
             wsp = keep.tile([P, P], U8, align_bytes=64, name="warm_stationary_plane")
-            nc.vector.memset(zero[:], 0.0)
+            nc.vector.memset(zero[:].bitcast(I32), 0)
             nc.vector.memset(g_plane[:].bitcast(I32), 0)
-            nc.vector.quantize_mx(out=wm[:].bitcast(E4M3X4), scales=wmp[:], in_=zero[:])
-            nc.vector.quantize_mx(out=ws[:].bitcast(E5M2X4), scales=wsp[:], in_=zero[:, : 4 * P])
+            for w in range(4):
+                cols = slice(w * P, (w + 1) * P)
+                nc.vector.quantize_mx(out=wm[:, cols].bitcast(E4M3X4), scales=wmp[:, cols], in_=zero[:])
+            nc.vector.quantize_mx(out=ws[:].bitcast(E5M2X4), scales=wsp[:], in_=zero[:])
             return wm, wmp, ws, wsp
 
         def warm(n):
             wm, wmp, ws, wsp = warm_tiles
-            bank = acc_psum.tile([P, PASS], F32, name="acc")
+            bank = psum.tile([P, PASS], F32, name="bank")
             for w in range(n):
                 nc.tensor.matmul_mx(out=bank[:], lhsT=ws[:].bitcast(E5M2X4), lhsT_scale=wsp[:], rhs=wm[:].bitcast(E4M3X4), rhs_scale=wmp[:], start=True, stop=True)
 
@@ -149,7 +150,7 @@ def tile_weighted_diis_residuals_e3_kernel(tc, g_words, g_scales, errs, pair, co
 
         def turn(j, g, rt):
             if (j, g, rt // 2) not in e_bank:
-                bank = turn_psum.tile([P, 4, P], F32, name="turn")
+                bank = psum.tile([P, 4, P], F32, name="bank")
                 e_bank[j, g, rt // 2] = bank
             for u in range(2):
                 if (j, rt, g // 2) in split:
@@ -175,7 +176,7 @@ def tile_weighted_diis_residuals_e3_kernel(tc, g_words, g_scales, errs, pair, co
 
         def overlap(j, i, g):
             if g == 0:
-                accs[j, i] = acc_psum.tile([P, PASS], F32, name="acc")
+                accs[j, i] = psum.tile([P, PASS], F32, name="bank")
             t, g0, i0 = g_code[i, g]
             nc.tensor.matmul_mx(
                 out=accs[j, i][:],
@@ -205,7 +206,7 @@ def tile_weighted_diis_residuals_e3_kernel(tc, g_words, g_scales, errs, pair, co
         def turn_h(j, i):
             q, a = divmod(i, 2)
             if (j, q) not in h_bank:
-                h_bank[j, q] = turn_psum.tile([P, 4, P], F32, name="turn")
+                h_bank[j, q] = psum.tile([P, 4, P], F32, name="bank")
             words = h_sb[j][i][:].bitcast(F32)
             for u in range(2):
                 nc.tensor.transpose(h_bank[j, q][:, 2 * a + u, :], words[:, u * P : (u + 1) * P], ident[:])
@@ -229,7 +230,7 @@ def tile_weighted_diis_residuals_e3_kernel(tc, g_words, g_scales, errs, pair, co
             )
 
         def zmm(i):
-            accs[2, i] = acc_psum.tile([P, PASS], F32, name="acc")
+            accs[2, i] = psum.tile([P, PASS], F32, name="bank")
             cols = slice((i % 2) * P, (i % 2 + 1) * P)
             for j in range(HALVES):
                 nc.tensor.matmul_mx(
@@ -254,176 +255,177 @@ def tile_weighted_diis_residuals_e3_kernel(tc, g_words, g_scales, errs, pair, co
             nc.vector.tensor_tensor(out=res[:], in0=accs[2, i][:], in1=lam_sb[:], op=ALU.subtract)
             nc.sync.dma_start(out=out[i * P : (i + 1) * P, :], in_=res[:])
 
-        warm(3)
-        turn(0, 1, 0)
+        warm(2)
         turn(0, 0, 0)
+        turn(0, 1, 0)
         turn(0, 2, 0)
         turn(0, 3, 0)
         warm(1)
         turn(0, 0, 1)
         turn(0, 1, 1)
-        turn(0, 3, 1)
         turn(0, 2, 1)
+        gather(0, 0, 0, "A")
+        turn(0, 3, 1)
         gather(0, 1, 0, "V")
-        gather(0, 3, 0, "A")
-        gather(0, 0, 0, "V")
+        gather(0, 2, 0, "A")
         warm(1)
         turn(0, 0, 2)
-        gather(0, 2, 0, "A")
-        quant(0, 0, 0)
-        turn(0, 0, 3)
-        quant(0, 1, 0)
-        turn(0, 3, 2)
+        gather(0, 3, 0, "V")
         turn(0, 1, 2)
-        gather(0, 0, 1, "V")
         turn(0, 2, 2)
-        turn(0, 2, 3)
+        turn(0, 3, 2)
+        quant(0, 0, 0)
+        quant(0, 1, 0)
+        turn(0, 0, 3)
         turn(0, 1, 3)
-        quant(0, 0, 1)
+        turn(0, 2, 3)
+        gather(0, 0, 1, "A")
         turn(0, 3, 3)
-        gather(0, 2, 1, "A")
         gather(0, 1, 1, "V")
+        gather(0, 2, 1, "A")
+        quant(0, 0, 1)
+        gather(0, 3, 1, "V")
+        warm(2)
         units(0, 0, "0")
-        gather(0, 3, 1, "A")
-        units(0, 3, "0")
-        quant(0, 2, 0)
-        units(0, 2, "0")
-        quant(0, 1, 1)
         units(0, 1, "0")
-        quant(0, 2, 1)
-        units(0, 0, "1")
+        quant(0, 1, 1)
+        units(0, 2, "0")
+        quant(0, 2, 0)
+        units(0, 3, "0")
         quant(0, 3, 0)
-        units(0, 3, "1")
+        units(0, 0, "1")
+        quant(0, 2, 1)
+        units(0, 1, "1")
         quant(0, 3, 1)
-        units(0, 0, "2")
         units(0, 2, "1")
+        units(0, 3, "1")
+        units(0, 0, "2")
+        units(0, 1, "2")
+        units(0, 2, "2")
         units(0, 3, "2")
         units(0, 0, "3")
-        units(0, 2, "2")
-        units(0, 2, "3")
-        units(0, 1, "1")
-        units(0, 3, "3")
-        weight(0, 0)
-        units(0, 1, "2")
         units(0, 1, "3")
-        weight(0, 3)
+        units(0, 2, "3")
+        weight(0, 0)
+        units(0, 3, "3")
         weight(0, 1)
         shuf(1, 0, 1, "A")
-        units(0, 4, "F")
-        weight(0, 2)
         shuf(1, 0, 0, "V")
+        units(0, 4, "F")
+        units(0, 5, "F")
         shuf(1, 1, 1, "A")
         shuf(1, 1, 0, "V")
-        units(0, 5, "F")
+        weight(0, 2)
+        turn(1, 0, 0)
+        turn(1, 0, 1)
         turn(1, 1, 0)
+        weight(0, 3)
+        turn(1, 1, 1)
+        gather(1, 0, 0, "A")
         turn(1, 2, 0)
         turn(1, 2, 1)
-        turn(1, 1, 1)
-        weight(0, 5)
         turn(1, 3, 0)
-        turn_h(0, 0)
-        turn(1, 3, 1)
         gather(1, 1, 0, "V")
-        turn_h(0, 1)
-        gather(1, 3, 0, "A")
-        gather(1, 2, 0, "V")
-        out_h(0, 0, "A")
-        shuf(1, 2, 0, "V")
-        units(0, 6, "F")
-        shuf(1, 2, 1, "V")
-        turn(1, 0, 0)
-        shuf(1, 3, 0, "V")
-        turn(1, 0, 2)
-        turn(1, 0, 1)
-        shuf(1, 3, 1, "V")
-        turn(1, 1, 2)
-        turn(1, 2, 2)
-        quant(1, 3, 0)
-        gather(1, 0, 0, "A")
-        turn(1, 1, 3)
-        turn(1, 2, 3)
+        turn(1, 3, 1)
+        gather(1, 2, 0, "A")
         weight(0, 4)
-        turn(1, 0, 3)
-        gather(1, 0, 1, "A")
-        gather(1, 2, 1, "V")
-        gather(1, 1, 1, "A")
-        quant(1, 0, 0)
-        units(0, 7, "F")
-        quant(1, 0, 1)
-        turn(1, 3, 2)
-        quant(1, 1, 0)
-        turn(1, 3, 3)
-        turn_h(0, 2)
-        quant(1, 1, 1)
-        turn_h(0, 4)
-        gather(1, 3, 1, "A")
-        turn_h(0, 5)
-        quant(1, 2, 0)
-        turn_h(0, 3)
-        quant(1, 2, 1)
-        out_h(0, 2, "A")
-        quant(1, 3, 1)
+        shuf(1, 2, 0, "A")
+        gather(1, 3, 0, "V")
+        units(0, 6, "F")
+        shuf(1, 2, 1, "A")
+        weight(0, 5)
+        turn(1, 0, 2)
+        turn(1, 1, 2)
+        shuf(1, 3, 1, "A")
+        shuf(1, 3, 0, "V")
+        turn(1, 2, 2)
         weight(0, 6)
-        units(1, 1, "F")
-        coef_copy(1, 0, "A")
-        coef_copy(0, 0, "V")
-        units(1, 3, "F")
-        weight(0, 7)
-        quant_h(0, 0)
-        coef_copy(0, 1, "A")
-        weight(1, 3)
-        units(1, 2, "F")
-        weight(1, 1)
-        coef_copy(1, 1, "A")
-        coef_quantize(0)
-        units(1, 5, "F")
-        weight(1, 2)
+        turn(1, 3, 2)
+        turn_h(0, 0)
+        turn_h(0, 1)
+        quant(1, 0, 0)
+        turn_h(0, 2)
+        turn_h(0, 3)
+        out_h(0, 0, "A")
+        quant(1, 1, 0)
+        turn(1, 0, 3)
+        turn(1, 1, 3)
+        quant(1, 2, 0)
+        turn(1, 2, 3)
+        turn(1, 3, 3)
+        gather(1, 0, 1, "A")
+        quant(1, 3, 0)
+        gather(1, 1, 1, "V")
+        gather(1, 2, 1, "A")
+        quant(1, 0, 1)
+        units(0, 7, "F")
+        gather(1, 3, 1, "A")
+        quant(1, 1, 1)
+        quant(1, 2, 1)
         out_h(0, 1, "A")
+        quant(1, 3, 1)
+        quant_h(0, 0)
         units(1, 0, "F")
-        coef_quantize(1)
-        weight(1, 0)
-        units(1, 7, "F")
+        weight(0, 7)
         quant_h(0, 1)
-        turn_h(1, 2)
-        weight(1, 5)
+        coef_copy(0, 1, "A")
+        weight(1, 0)
+        units(1, 1, "F")
+        turn_h(0, 4)
+        turn_h(0, 5)
+        weight(1, 1)
         turn_h(0, 6)
-        turn_h(1, 3)
         turn_h(0, 7)
-        turn_h(1, 0)
-        weight(1, 7)
-        turn_h(1, 1)
+        out_h(0, 2, "A")
+        coef_copy(0, 0, "V")
+        out_h(0, 3, "A")
         quant_h(0, 2)
+        units(1, 2, "F")
+        coef_copy(1, 1, "A")
+        quant_h(0, 3)
+        weight(1, 2)
+        units(1, 3, "F")
+        coef_quantize(0)
+        weight(1, 3)
+        units(1, 4, "F")
+        coef_copy(1, 0, "V")
+        weight(1, 4)
+        units(1, 5, "F")
+        coef_quantize(1)
+        turn_h(1, 0)
+        turn_h(1, 1)
+        turn_h(1, 2)
+        turn_h(1, 3)
+        weight(1, 5)
         out_h(1, 0, "A")
         out_h(1, 1, "A")
-        units(1, 6, "F")
         quant_h(1, 0)
-        out_h(0, 3, "A")
+        units(1, 6, "F")
+        quant_h(1, 1)
         weight(1, 6)
-        units(1, 4, "F")
-        quant_h(0, 3)
+        units(1, 7, "F")
         zmm(0)
-        weight(1, 4)
-        turn_h(1, 6)
-        turn_h(1, 7)
+        weight(1, 7)
+        zmm(1)
         store(0)
         turn_h(1, 4)
         turn_h(1, 5)
-        out_h(1, 3, "A")
-        quant_h(1, 1)
-        zmm(1)
-        out_h(1, 2, "A")
-        quant_h(1, 3)
-        zmm(3)
         store(1)
-        zmm(7)
-        quant_h(1, 2)
-        store(3)
-        zmm(4)
-        store(7)
+        turn_h(1, 6)
+        turn_h(1, 7)
+        out_h(1, 2, "A")
         zmm(2)
-        store(4)
-        zmm(5)
+        out_h(1, 3, "A")
+        quant_h(1, 2)
+        zmm(3)
+        quant_h(1, 3)
+        zmm(4)
         store(2)
+        zmm(5)
+        store(3)
         zmm(6)
+        store(4)
+        zmm(7)
         store(5)
-        store_last(6)
+        store(6)
+        store_last(7)

from contextlib import ExitStack

import concourse.mybir as mybir
from concourse.masks import make_identity

M, K, R = 1024, 2048, 512
FLOPS = 2 * M * M * K + 2 * M * M * R
BYTES = K * M + K * M // 32 + 2 * M * K + 2 * M * M + 2 * M * R + 2 * R + 4 * M * R

F32 = mybir.dt.float32
BF16 = mybir.dt.bfloat16
U32 = mybir.dt.uint32
I32 = mybir.dt.int32
U8 = mybir.dt.uint8
E4M3X4 = mybir.dt.float8_e4m3fn_x4
E5M2X4 = mybir.dt.float8_e5m2_x4
ALU = mybir.AluOpType

P = 128
PASS = 512
GROUPS = K // PASS
HALVES = M // PASS
TILES = M // P
BLOCKS = PASS // P


def tile_weighted_diis_residuals_e3_kernel(tc, g_words, g_scales, errs, pair, coef, lam, out):
    nc = tc.nc
    with ExitStack() as ctx:
        keep = ctx.enter_context(tc.tile_pool(name="keep", bufs=1))
        stage = ctx.enter_context(tc.tile_pool(name="stage", bufs=4))
        psum = ctx.enter_context(tc.psum_pool(name="psum", bufs=8))
        ctx.enter_context(tc.manual_schedule())

        g_code = {}
        g_plane = keep.tile([P, GROUPS, M], U8, align_bytes=64, name="g_plane")
        pair_sb = {}
        coef_raw = keep.tile([P, HALVES, 4, R], BF16, align_bytes=64, name="coef_raw")
        coef_quads = [keep.tile([P, R, 4], BF16, align_bytes=64, name=f"coef_quads{j}") for j in range(HALVES)]
        coef_code = [keep.tile([P, R], U32, align_bytes=64, name=f"coef_code{j}") for j in range(HALVES)]
        coef_plane = [keep.tile([P, R], U8, align_bytes=64, name=f"coef_plane{j}") for j in range(HALVES)]
        lam_sb = keep.tile([P, R], BF16, align_bytes=64, name="lam_sb")
        ident = keep.tile([P, P], F32, align_bytes=64, name="ident")
        e_code = [[keep.tile([P, PASS], U32, align_bytes=64, name=f"e_code{j}{g}") for g in range(GROUPS)] for j in range(HALVES)]
        e_plane = [[keep.tile([P, PASS], U8, align_bytes=64, name=f"e_plane{j}{g}") for g in range(GROUPS)] for j in range(HALVES)]
        h_code = [[keep.tile([P, 2 * P], U32, align_bytes=64, name=f"h_code{j}{q}") for q in range(4)] for j in range(HALVES)]
        h_plane = [[keep.tile([P, 2 * P], U8, align_bytes=64, name=f"h_plane{j}{q}") for q in range(4)] for j in range(HALVES)]
        h_sb = [[keep.tile([P, PASS], BF16, align_bytes=64, name=f"h{j}{i}") for i in range(TILES)] for j in range(HALVES)]

        make_identity(nc, ident[:])

        def warm_setup():
            zero = keep.tile([P, PASS], BF16, align_bytes=64, name="zero")
            wm = keep.tile([P, PASS], U32, align_bytes=64, name="warm_moving")
            wmp = keep.tile([P, PASS], U8, align_bytes=64, name="warm_moving_plane")
            ws = keep.tile([P, P], U32, align_bytes=64, name="warm_stationary")
            wsp = keep.tile([P, P], U8, align_bytes=64, name="warm_stationary_plane")
            nc.vector.memset(zero[:].bitcast(I32), 0)
            nc.vector.memset(g_plane[:].bitcast(I32), 0)
            for w in range(4):
                cols = slice(w * P, (w + 1) * P)
                nc.vector.quantize_mx(out=wm[:, cols].bitcast(E4M3X4), scales=wmp[:, cols], in_=zero[:])
            nc.vector.quantize_mx(out=ws[:].bitcast(E5M2X4), scales=wsp[:], in_=zero[:])
            return wm, wmp, ws, wsp

        def warm(n):
            wm, wmp, ws, wsp = warm_tiles
            bank = psum.tile([P, PASS], F32, name="bank")
            for w in range(n):
                nc.tensor.matmul_mx(out=bank[:], lhsT=ws[:].bitcast(E5M2X4), lhsT_scale=wsp[:], rhs=wm[:].bitcast(E4M3X4), rhs_scale=wmp[:], start=True, stop=True)

        warm_tiles = warm_setup()

        e_raw = {}

        def load_errs(j, rt):
            t = keep.tile([P, K], BF16, align_bytes=64, name=f"e_raw{j}{rt}")
            nc.sync.dma_start(out=t[:], in_=errs[j * PASS + rt * P : j * PASS + (rt + 1) * P, :])
            e_raw[j, rt] = t

        def load_g(i0, ni, g0, ng):
            t = keep.tile([P, ng, ni * P], U32, align_bytes=64, name=f"g_code{i0}{g0}")
            nc.sync.dma_start(
                out=t[:].bitcast(I32),
                in_=g_words[g0 : g0 + ng].rearrange("g p n t -> p g (n t)")[:, :, i0 * 4 * P : (i0 + ni) * 4 * P].bitcast(I32),
            )
            for i in range(i0, i0 + ni):
                for g in range(g0, g0 + ng):
                    g_code[i, g] = (t, g0, i0)
        def load_scales():
            for quad in range(4):
                nc.sync.dma_start(
                    out=g_plane[32 * quad : 32 * quad + 4, :, :].bitcast(I32),
                    in_=g_scales[:, 4 * quad : 4 * quad + 4, :].rearrange("g r n -> r g n").bitcast(I32),
                )

        def load_pair(h, j):
            pair_sb[h, j] = keep.tile([P, BLOCKS, PASS], BF16, align_bytes=64, name=f"pair{h}{j}")
            nc.sync.dma_start(
                out=pair_sb[h, j][:],
                in_=pair[h * PASS : (h + 1) * PASS, j * PASS : (j + 1) * PASS].rearrange("(i p) j -> p i j", p=P),
            )

        def load_coef():
            nc.sync.dma_start(out=coef_raw[:], in_=coef.rearrange("(j p t) r -> p j t r", p=P, t=4))

        def load_lam():
            nc.sync.dma_start(out=lam_sb[:], in_=lam.partition_broadcast(P))

        load_errs(0, 0)
        load_scales()
        load_errs(0, 1)
        load_errs(0, 2)
        load_errs(0, 3)
        load_g(0, 8, 0, 1)
        load_g(0, 8, 1, 1)
        load_g(0, 8, 2, 1)
        load_g(0, 8, 3, 1)
        load_pair(0, 0)
        load_errs(1, 0)
        load_errs(1, 1)
        load_pair(1, 0)
        load_errs(1, 2)
        load_errs(1, 3)
        load_pair(0, 1)
        load_pair(1, 1)
        load_coef()
        load_lam()

        split = {}
        e_quads = {}

        def move(engine, dst, src):
            if engine == "V":
                nc.vector.tensor_copy(out=dst, in_=src)
            else:
                nc.scalar.copy(out=dst, in_=src)

        def quad_words(quads, col):
            words = quads.rearrange("p n t -> p (n t)").bitcast(F32)
            return words[:, 2 * col : 2 * (col + 2 * P)].rearrange("p (b r u) -> p b r u", b=2, u=2)

        e_bank = {}

        def shuf(j, rt, kh, engine):
            t = stage.tile([P, 2, 2, P], F32, align_bytes=64, name="split", bufs=8)
            src = e_raw[j, rt][:].bitcast(F32)[:, kh * PASS : (kh + 1) * PASS].rearrange("p (g w u) -> p g u w", g=2, u=2)
            move(engine, t[:], src)
            split[j, rt, kh] = t

        def turn(j, g, rt):
            if (j, g, rt // 2) not in e_bank:
                bank = psum.tile([P, 4, P], F32, name="bank")
                e_bank[j, g, rt // 2] = bank
            for u in range(2):
                if (j, rt, g // 2) in split:
                    word = split[j, rt, g // 2][:, g % 2, u, :]
                else:
                    word = e_raw[j, rt][:].bitcast(F32)[:, 2 * P * g + u : 2 * P * (g + 1) : 2]
                nc.tensor.transpose(e_bank[j, g, rt // 2][:, 2 * (rt % 2) + u, :], word, ident[:])

        def gather(j, g, c, engine):
            if (j, g) not in e_quads:
                e_quads[j, g] = keep.tile([P, PASS, 4], BF16, align_bytes=64, name=f"e_quads{j}{g}")
            move(engine, quad_words(e_quads[j, g][:], 2 * c * P), e_bank[j, g, c][:].rearrange("p (b u) r -> p b r u", u=2))

        def quant(j, g, c):
            cols = slice(2 * c * P, 2 * (c + 1) * P)
            nc.vector.quantize_mx(
                out=e_code[j][g][:, cols].bitcast(E4M3X4),
                scales=e_plane[j][g][:, cols],
                in_=e_quads[j, g][:, cols, :].rearrange("p n t -> p (n t)"),
            )

        accs = {}

        def overlap(j, i, g):
            if g == 0:
                accs[j, i] = psum.tile([P, PASS], F32, name="bank")
            t, g0, i0 = g_code[i, g]
            nc.tensor.matmul_mx(
                out=accs[j, i][:],
                lhsT=t[:, g - g0, (i - i0) * P : (i - i0 + 1) * P].bitcast(E5M2X4),
                lhsT_scale=g_plane[:, g, i * P : (i + 1) * P],
                rhs=e_code[j][g][:].bitcast(E4M3X4),
                rhs_scale=e_plane[j][g][:],
                start=(g == 0),
                stop=(g == GROUPS - 1),
            )

        def units(j, i, part):
            for g in {"F": (0, 1, 2, 3), "0": (0,), "1": (1,), "2": (2,), "3": (3,)}[part]:
                overlap(j, i, g)

        def weight(j, i):
            nc.vector.tensor_tensor(
                out=h_sb[j][i][:].rearrange("p (u w e) -> p u w e", u=2, e=2),
                in0=accs[j, i][:].rearrange("p (w u e) -> p u w e", u=2, e=2),
                in1=pair_sb[i // BLOCKS, j][:, i % BLOCKS, :].rearrange("p (w u e) -> p u w e", u=2, e=2),
                op=ALU.mult,
            )

        h_bank = {}
        h_quads = {}

        def turn_h(j, i):
            q, a = divmod(i, 2)
            if (j, q) not in h_bank:
                h_bank[j, q] = psum.tile([P, 4, P], F32, name="bank")
            words = h_sb[j][i][:].bitcast(F32)
            for u in range(2):
                nc.tensor.transpose(h_bank[j, q][:, 2 * a + u, :], words[:, u * P : (u + 1) * P], ident[:])

        def out_h(j, q, engine="A"):
            h_quads[j, q] = stage.tile([P, 2 * P, 4], BF16, align_bytes=64, name="h_quads", bufs=8)
            move(engine, quad_words(h_quads[j, q][:], 0), h_bank[j, q][:].rearrange("p (b u) r -> p b r u", u=2))

        def quant_h(j, q):
            nc.vector.quantize_mx(
                out=h_code[j][q][:].bitcast(E5M2X4), scales=h_plane[j][q][:], in_=h_quads[j, q][:].rearrange("p n t -> p (n t)")
            )

        def coef_copy(j, c, engine="A"):
            cols = slice(c * R // 2, (c + 1) * R // 2)
            move(engine, coef_quads[j][:, cols, :], coef_raw[:, j, :, cols].rearrange("p t n -> p n t"))

        def coef_quantize(j):
            nc.vector.quantize_mx(
                out=coef_code[j][:].bitcast(E4M3X4), scales=coef_plane[j][:], in_=coef_quads[j][:].rearrange("p n t -> p (n t)")
            )

        def zmm(i):
            accs[2, i] = psum.tile([P, PASS], F32, name="bank")
            cols = slice((i % 2) * P, (i % 2 + 1) * P)
            for j in range(HALVES):
                nc.tensor.matmul_mx(
                    out=accs[2, i][:],
                    lhsT=h_code[j][i // 2][:, cols].bitcast(E5M2X4),
                    lhsT_scale=h_plane[j][i // 2][:, cols],
                    rhs=coef_code[j][:].bitcast(E4M3X4),
                    rhs_scale=coef_plane[j][:],
                    start=(j == 0),
                    stop=(j == HALVES - 1),
                )

        def store_last(i):
            for c in range(2):
                cols = slice(c * R // 2, (c + 1) * R // 2)
                res = keep.tile([P, R // 2], F32, align_bytes=64, name=f"res_last{c}")
                nc.vector.tensor_tensor(out=res[:], in0=accs[2, i][:, cols], in1=lam_sb[:, cols], op=ALU.subtract)
                nc.sync.dma_start(out=out[i * P : (i + 1) * P, cols], in_=res[:])

        def store(i):
            res = keep.tile([P, R], F32, align_bytes=64, name=f"res{i}")
            nc.vector.tensor_tensor(out=res[:], in0=accs[2, i][:], in1=lam_sb[:], op=ALU.subtract)
            nc.sync.dma_start(out=out[i * P : (i + 1) * P, :], in_=res[:])

        warm(2)
        turn(0, 0, 0)
        turn(0, 1, 0)
        turn(0, 2, 0)
        turn(0, 3, 0)
        warm(1)
        turn(0, 0, 1)
        turn(0, 1, 1)
        turn(0, 2, 1)
        gather(0, 0, 0, "A")
        turn(0, 3, 1)
        gather(0, 1, 0, "V")
        gather(0, 2, 0, "A")
        warm(1)
        turn(0, 0, 2)
        gather(0, 3, 0, "V")
        turn(0, 1, 2)
        turn(0, 2, 2)
        turn(0, 3, 2)
        quant(0, 0, 0)
        quant(0, 1, 0)
        turn(0, 0, 3)
        turn(0, 1, 3)
        turn(0, 2, 3)
        gather(0, 0, 1, "A")
        turn(0, 3, 3)
        gather(0, 1, 1, "V")
        gather(0, 2, 1, "A")
        quant(0, 0, 1)
        gather(0, 3, 1, "V")
        warm(2)
        units(0, 0, "0")
        units(0, 1, "0")
        quant(0, 1, 1)
        units(0, 2, "0")
        quant(0, 2, 0)
        units(0, 3, "0")
        quant(0, 3, 0)
        units(0, 0, "1")
        quant(0, 2, 1)
        units(0, 1, "1")
        quant(0, 3, 1)
        units(0, 2, "1")
        units(0, 3, "1")
        units(0, 0, "2")
        units(0, 1, "2")
        units(0, 2, "2")
        units(0, 3, "2")
        units(0, 0, "3")
        units(0, 1, "3")
        units(0, 2, "3")
        weight(0, 0)
        units(0, 3, "3")
        weight(0, 1)
        shuf(1, 0, 1, "A")
        shuf(1, 0, 0, "V")
        units(0, 4, "F")
        units(0, 5, "F")
        shuf(1, 1, 1, "A")
        shuf(1, 1, 0, "V")
        weight(0, 2)
        turn(1, 0, 0)
        turn(1, 0, 1)
        turn(1, 1, 0)
        weight(0, 3)
        turn(1, 1, 1)
        gather(1, 0, 0, "A")
        turn(1, 2, 0)
        turn(1, 2, 1)
        turn(1, 3, 0)
        gather(1, 1, 0, "V")
        turn(1, 3, 1)
        gather(1, 2, 0, "A")
        weight(0, 4)
        shuf(1, 2, 0, "A")
        gather(1, 3, 0, "V")
        units(0, 6, "F")
        shuf(1, 2, 1, "A")
        weight(0, 5)
        turn(1, 0, 2)
        turn(1, 1, 2)
        shuf(1, 3, 1, "A")
        shuf(1, 3, 0, "V")
        turn(1, 2, 2)
        weight(0, 6)
        turn(1, 3, 2)
        turn_h(0, 0)
        turn_h(0, 1)
        quant(1, 0, 0)
        turn_h(0, 2)
        turn_h(0, 3)
        out_h(0, 0, "A")
        quant(1, 1, 0)
        turn(1, 0, 3)
        turn(1, 1, 3)
        quant(1, 2, 0)
        turn(1, 2, 3)
        turn(1, 3, 3)
        gather(1, 0, 1, "A")
        quant(1, 3, 0)
        gather(1, 1, 1, "V")
        gather(1, 2, 1, "A")
        quant(1, 0, 1)
        units(0, 7, "F")
        gather(1, 3, 1, "A")
        quant(1, 1, 1)
        quant(1, 2, 1)
        out_h(0, 1, "A")
        quant(1, 3, 1)
        quant_h(0, 0)
        units(1, 0, "F")
        weight(0, 7)
        quant_h(0, 1)
        coef_copy(0, 1, "A")
        weight(1, 0)
        units(1, 1, "F")
        turn_h(0, 4)
        turn_h(0, 5)
        weight(1, 1)
        turn_h(0, 6)
        turn_h(0, 7)
        out_h(0, 2, "A")
        coef_copy(0, 0, "V")
        out_h(0, 3, "A")
        quant_h(0, 2)
        units(1, 2, "F")
        coef_copy(1, 1, "A")
        quant_h(0, 3)
        weight(1, 2)
        units(1, 3, "F")
        coef_quantize(0)
        weight(1, 3)
        units(1, 4, "F")
        coef_copy(1, 0, "V")
        weight(1, 4)
        units(1, 5, "F")
        coef_quantize(1)
        turn_h(1, 0)
        turn_h(1, 1)
        turn_h(1, 2)
        turn_h(1, 3)
        weight(1, 5)
        out_h(1, 0, "A")
        out_h(1, 1, "A")
        quant_h(1, 0)
        units(1, 6, "F")
        quant_h(1, 1)
        weight(1, 6)
        units(1, 7, "F")
        zmm(0)
        weight(1, 7)
        zmm(1)
        store(0)
        turn_h(1, 4)
        turn_h(1, 5)
        store(1)
        turn_h(1, 6)
        turn_h(1, 7)
        out_h(1, 2, "A")
        zmm(2)
        out_h(1, 3, "A")
        quant_h(1, 2)
        zmm(3)
        quant_h(1, 3)
        zmm(4)
        store(2)
        zmm(5)
        store(3)
        zmm(6)
        store(4)
        zmm(7)
        store(5)
        store(6)
        store_last(7)
